import numpy as np, ml_dtypes
CORES = [2,3,42,43,82,83,122,123]
N = 8
import mx_ref
KO = 3
F = np.float32(0.8)
OWN = [5,5,5,5,5,5,5,5]
BF = ml_dtypes.bfloat16
def tile(rs):
    return np.stack(rs, axis=2).reshape(128, -1).astype(BF)
def pick(b):
    s = np.zeros((128, 128, 4), np.float32)
    s[np.arange(128), np.arange(128), b] = 1.0
    return mx_ref.quantize(s.reshape(128, 512).astype(BF))
def pk(c, s, i=0):
    return (np.ascontiguousarray(c[:, 512 * i:512 * i + 512]), mx_ref.live(s[:, 128 * i:128 * i + 128]))
def inputs(rng, e, E):
    def f(*shape):
        v = (rng.standard_normal(shape, dtype=np.float32) * np.exp2(rng.integers(-2, 3, shape[:-1] + (1,)))).astype(BF)
        return mx_ref.spread((v.astype(np.float32) * np.exp2(rng.integers(-E, E + 1, shape[:-2] + (1, 1))).astype(np.float32)).astype(BF), rng, e)
    def packed(k):
        c = np.zeros((N, 128, k * 512), np.uint8); s = np.zeros((N, 128, k * 128), np.uint8)
        for r in range(N):
            for i in range(k):
                a, b = mx_ref.quantize(f(128, 512)); c[r][:, 512 * i:512 * i + 512] = a; s[r][:, 128 * i:128 * i + 128] = mx_ref.plane(b, rng)
        return c, s
    d = {}
    d["kc"], d["ks"] = packed(KO)
    d["q"] = f(N, 128, 512)
    return d
def setup_inputs(rng):
    return inputs(rng, 0, 0)
def setup_inputs_blocks(rng):
    return inputs(rng, 4, 0)
def setup_inputs_wide(rng):
    return inputs(rng, 0, 8)
def reference(kc, ks, q):
    S = [pick(t) for t in range(4)]
    anew = lambda p, i: mx_ref.quantize(tile([mx_ref.matmul(S[t], pk(kc[p], ks[p], i)) * F for t in range(4)]))
    y = np.full((N, 128, 3072), np.nan, np.float32)
    for o in range(N):
        if OWN[o] != o: continue
        qq = mx_ref.quantize(q[o])
        M = [pk(kc[o], ks[o], i) for i in range(KO)] + [anew(p, i) for p in range(N) if p != o and OWN[p] == o for i in range(KO)]
        y[o][:, :128 * len(M)] = np.concatenate([mx_ref.matmul(qq, m) for m in M], axis=1)
    return {"y": y}

@@ -1,0 +1,158 @@
+from concourse.mybir import dt, AluOpType, ActivationFunctionType
+
+N = 8
+KO = 3
+C = 128
+W = KO * C
+PIECES = [(0, 2), (2, 3)]
+FAC = 0.800000011920929
+X4 = "float8_e4m3fn_x4"
+
+SCRATCH = {
+    "kcb": ("sbuf", [128, W], X4),
+    "ksb": ("sbuf", [128, W], "uint8"),
+    "strip": ("sbuf", [128, 516], "bfloat16"),
+    "sc": ("sbuf", [128, 4 * C], X4),
+    "ss": ("sbuf", [128, 4 * C], "uint8"),
+    "h": ("sbuf", [128, 4 * W], "bfloat16"),
+    "nc": ("sbuf", [128, W], X4),
+    "ns": ("sbuf", [128, W], "uint8"),
+    "lc": ("sbuf", [128, (N - 1) * W], X4),
+    "ls": ("sbuf", [128, (N - 1) * W], "uint8"),
+    "qb": ("sbuf", [128, 4 * C], "bfloat16"),
+    "qc": ("sbuf", [128, C], X4),
+    "qs": ("sbuf", [128, C], "uint8"),
+    "yb": ("sbuf", [128, N * W], "float32"),
+}
+for _k in range(8):
+    SCRATCH["ps%d" % _k] = ("psum", [128, 512], "float32")
+
+SEMAPHORES = ["ld0", "ld1", "ldp", "ldq", "fill", "diag", "sel", "mm", "vm", "sm", "qd", "sent", "st0", "st1"]
+SEMAPHORES += ["a%d_%d" % (_p, _i) for _p in range(N) for _i in range(len(PIECES))]
+
+
+def bits(m):
+    return bin(m).count("1")
+
+
+def producer(g, core, T, topo, slot, dst, rank):
+    Copy = ActivationFunctionType.Copy
+    S = T.sem
+    g.sync.dma_start(T.kcb[:, 0:C].bitcast(dt.uint8), T.kc[:, 0:4 * C]).then_inc(S.ld0, 16)
+    g.scalar.dma_start(T.ksb[:], T.ks[:]).then_inc(S.ldp, 16)
+    g.sync.dma_start(T.kcb[:, C:W].bitcast(dt.uint8), T.kc[:, 4 * C:4 * W]).then_inc(S.ld1, 16)
+    g.vector.memset(T.strip[:], 0.0).then_inc(S.fill, 1)
+    g.wait_ge(S.fill, 1)
+    d = T.strip[:, 3:515:4]
+    g.affine_select(d, d, [[-1, C]], AluOpType.not_equal, 1.0, 0, 1).then_inc(S.diag, 1)
+    g.vector.wait_ge(S.diag, 1)
+    order = (0, 2, 1, 3)
+    for b in order:
+        g.vector.quantize_mx(T.sc[:, C * b:C * b + C], T.ss[:, C * b:C * b + C], T.strip[:, 3 - b:515 - b]).then_inc(S.sel, 1)
+    for c in range(KO):
+        if c == 0:
+            g.tensor.wait_ge(S.ld0, 16)
+            g.tensor.wait_ge(S.ldp, 16)
+        if c == 1:
+            g.tensor.wait_ge(S.ld1, 16)
+        if c >= 2:
+            g.tensor.wait_ge(S.vm, 2 * (c - 1))
+            g.tensor.wait_ge(S.sm, 2 * (c - 1))
+        cols = slice(C * c, C * c + C)
+        for k, b in enumerate(order):
+            if c == 0:
+                g.tensor.wait_ge(S.sel, k + 1)
+            g.tensor.matmul_mx(T["ps%d" % (4 * (c % 2) + b)][:, 0:C], T.sc[:, C * b:C * b + C], T.ss[:, C * b:C * b + C],
+                               T.kcb[:, cols], T.ksb[:, cols], True, True).then_inc(S.mm, 1)
+        for k, b in enumerate(order):
+            src = T["ps%d" % (4 * (c % 2) + b)][:, 0:C]
+            out = T.h[:, 4 * C * c + b:4 * C * (c + 1):4]
+            if b < 2:
+                g.scalar.wait_ge(S.mm, 4 * c + k + 1)
+                g.scalar.activation(out, src, Copy, scale=FAC).then_inc(S.sm, 1)
+            else:
+                g.vector.wait_ge(S.mm, 4 * c + k + 1)
+                g.vector.tensor_scalar(out, src, FAC, None, AluOpType.mult).then_inc(S.vm, 1)
+        g.vector.wait_ge(S.vm, 2 * (c + 1))
+        g.vector.wait_ge(S.sm, 2 * (c + 1))
+        g.vector.quantize_mx(T.nc[:, cols], T.ns[:, cols], T.h[:, 4 * C * c:4 * C * (c + 1)]).then_inc(S.qd, 1)
+    rid, pid, _ = topo.addr(dst)
+    mask = topo.mask(core, dst)
+    total = 0
+    for i, (a, b) in enumerate(PIECES):
+        g.wait_ge(S.qd, b)
+        here = slice(C * a, C * b)
+        there = slice(W * slot + C * a, W * slot + C * b)
+        arr = T.sem["a%d_%d" % (rank, i)]
+        g.remote_dma(out_ap=T.lc[:, there].bitcast(dt.uint8), in_ap=T.nc[:, here].bitcast(dt.uint8), remote_sem=arr,
+                     local_sem=S.sent, pid=pid, routing_id=rid, dma_engine_mask=mask)
+        g.remote_dma(out_ap=T.ls[:, there], in_ap=T.ns[:, here], remote_sem=arr,
+                     local_sem=S.sent, pid=pid, routing_id=rid, dma_engine_mask=mask)
+        total += 2 * bits(mask)
+    g.wait_ge(S.sent, total)
+
+
+def consumer(g, core, T, topo, rank, prods):
+    Copy = ActivationFunctionType.Copy
+    S = T.sem
+    g.sync.dma_start(T.qb[:], T.q[:]).then_inc(S.ldq, 16)
+    g.scalar.dma_start(T.ksb[:], T.ks[:]).then_inc(S.ldp, 16)
+    g.sync.dma_start(T.kcb[:].bitcast(dt.uint8), T.kc[:]).then_inc(S.ld0, 16)
+    g.vector.wait_ge(S.ldq, 16)
+    g.vector.quantize_mx(T.qc[:], T.qs[:], T.qb[:]).then_inc(S.qd, 1)
+    g.tensor.wait_ge(S.qd, 1)
+    work = [(None, 0, KO, [(S.ldp, 16), (S.ld0, 16)])]
+    near = [p for p in prods if topo.chip(T.cores[p]) == topo.chip(core)]
+    far = [p for p in prods if p not in near]
+    for group in (near, far):
+        for i, (a, b) in enumerate(PIECES):
+            for p in group:
+                n = 2 * bits(topo.mask(T.cores[p], core))
+                work.append((p, a, b, [(T.sem["a%d_%d" % (p, i)], n)]))
+    nv, ns, stores, u = 0, 0, [0, 0], 0
+    for k, (p, a, b, waits) in enumerate(work):
+        for s, v in waits:
+            g.tensor.wait_ge(s, v)
+        if p is None:
+            kc, ks, base, ybase = T.kcb, T.ksb, 0, 0
+        else:
+            kc, ks, base = T.lc, T.ls, W * prods.index(p)
+            ybase = W + base
+        for c in range(a, b):
+            if u >= 8:
+                g.tensor.wait_ge(S.vm if u % 2 == 0 else S.sm, (u - 8) // 2 + 1)
+            ps = T["ps%d" % (u % 8)][:, 0:C]
+            cols = slice(base + C * c, base + C * c + C)
+            g.tensor.matmul_mx(ps, T.qc[:], T.qs[:], kc[:, cols], ks[:, cols], True, True).then_inc(S.mm, 1)
+            out = T.yb[:, ybase + C * c:ybase + C * c + C]
+            if u % 2 == 0:
+                g.vector.wait_ge(S.mm, u + 1)
+                g.vector.tensor_copy(out, ps).then_inc(S.vm, 1)
+                nv += 1
+            else:
+                g.scalar.wait_ge(S.mm, u + 1)
+                g.scalar.activation(out, ps, Copy).then_inc(S.sm, 1)
+                ns += 1
+            u += 1
+        j = (u - 1) % 2 if b - a == 1 else k % 2
+        queue = g.scalar if j else g.sync
+        queue.wait_ge(S.vm, nv)
+        queue.wait_ge(S.sm, ns)
+        ycols = slice(ybase + C * a, ybase + C * b)
+        queue.dma_start(T.y[:, ycols], T.yb[:, ycols]).then_inc(S.st1 if j else S.st0, 16)
+        stores[j] += 16
+    g.sync.wait_ge(S.st0, stores[0])
+    g.scalar.wait_ge(S.st1, stores[1])
+
+
+def rank_program(g, core, T, topo):
+    rank = T.rank_of(core)
+    if rank is None:
+        return
+    own = T.tables["OWN"]
+    o = own[rank]
+    prods = [p for p in range(N) if p != o and own[p] == o]
+    if o == rank:
+        consumer(g, core, T, topo, rank, prods)
+    else:
+        producer(g, core, T, topo, prods.index(rank), T.cores[o], rank)

@@ -4,7 +4,7 @@ N = 8
 KO = 3
 C = 128
 W = KO * C
-PIECES = [(0, 2), (2, 3)]
+SIM = 128
 FAC = 0.800000011920929
 X4 = "float8_e4m3fn_x4"
 
@@ -28,14 +28,54 @@ for _k in range(8):
     SCRATCH["ps%d" % _k] = ("psum", [128, 512], "float32")
 
 SEMAPHORES = ["ld0", "ld1", "ldp", "ldq", "fill", "diag", "sel", "mm", "vm", "sm", "qd", "sent", "st0", "st1"]
-SEMAPHORES += ["a%d_%d" % (_p, _i) for _p in range(N) for _i in range(len(PIECES))]
+SEMAPHORES += ["c%d_%d" % (_p, _i) for _p in range(N) for _i in range(KO)] + ["p%d" % _p for _p in range(N)]
+
+NEAR = [("c", 0, 3, False), ("p", 0, 3, False)]
+STRAIGHT = [("c", 0, 1, False), ("p", 0, 3, False), ("c", 1, 2, False), ("c", 2, 3, False)]
+SPLIT = [("c", 0, 1, True), ("p", 0, 3, True), ("c", 1, 2, True), ("c", 2, 3, False)]
 
 
 def bits(m):
     return bin(m).count("1")
 
 
-def producer(g, core, T, topo, slot, dst, rank):
+def plan(T, topo, o):
+    own = T.tables["OWN"]
+    dst = T.cores[o]
+    prods = [p for p in range(N) if p != o and own[p] == o]
+    writes, via, seen = {}, {}, {}
+    for p in prods:
+        c = T.cores[p]
+        if topo.chip(c) == topo.chip(dst):
+            writes[p] = NEAR
+            continue
+        writes[p] = STRAIGHT
+        place = (topo.chip(c), topo.die(c))
+        seen[place] = seen.get(place, 0) + 1
+        if seen[place] % 2 == 1:
+            free = [x for x in range(SIM) if topo.chip(x) == topo.chip(c) and topo.die(x) != topo.die(c)
+                    and topo.may_write(x, dst) and T.rank_of(x) is None and x not in via.values()]
+            if free:
+                writes[p], via[p] = SPLIT, free[0]
+    return prods, writes, via
+
+
+def send(g, T, topo, core, to, mask, slot, rank, write, landed):
+    kind, a, b, _ = write
+    there = slice(W * slot + C * a, W * slot + C * b)
+    here = there if landed else slice(C * a, C * b)
+    rid, pid, _ = topo.addr(to)
+    if kind == "c":
+        src = T.lc if landed else T.nc
+        out, in_, sem = T.lc[:, there].bitcast(dt.uint8), src[:, here].bitcast(dt.uint8), T.sem["c%d_%d" % (rank, a)]
+    else:
+        src = T.ls if landed else T.ns
+        out, in_, sem = T.ls[:, there], src[:, here], T.sem["p%d" % rank]
+    g.remote_dma(out_ap=out, in_ap=in_, remote_sem=sem, local_sem=T.sem.sent, pid=pid, routing_id=rid, dma_engine_mask=mask)
+    return bits(mask)
+
+
+def producer(g, core, T, topo, slot, dst, rank, writes, via):
     Copy = ActivationFunctionType.Copy
     S = T.sem
     g.sync.dma_start(T.kcb[:, 0:C].bitcast(dt.uint8), T.kc[:, 0:4 * C]).then_inc(S.ld0, 16)
@@ -76,23 +116,26 @@ def producer(g, core, T, topo, slot, dst, rank):
         g.vector.wait_ge(S.vm, 2 * (c + 1))
         g.vector.wait_ge(S.sm, 2 * (c + 1))
         g.vector.quantize_mx(T.nc[:, cols], T.ns[:, cols], T.h[:, 4 * C * c:4 * C * (c + 1)]).then_inc(S.qd, 1)
-    rid, pid, _ = topo.addr(dst)
     mask = topo.mask(core, dst)
     total = 0
-    for i, (a, b) in enumerate(PIECES):
-        g.wait_ge(S.qd, b)
-        here = slice(C * a, C * b)
-        there = slice(W * slot + C * a, W * slot + C * b)
-        arr = T.sem["a%d_%d" % (rank, i)]
-        g.remote_dma(out_ap=T.lc[:, there].bitcast(dt.uint8), in_ap=T.nc[:, here].bitcast(dt.uint8), remote_sem=arr,
-                     local_sem=S.sent, pid=pid, routing_id=rid, dma_engine_mask=mask)
-        g.remote_dma(out_ap=T.ls[:, there], in_ap=T.ns[:, here], remote_sem=arr,
-                     local_sem=S.sent, pid=pid, routing_id=rid, dma_engine_mask=mask)
-        total += 2 * bits(mask)
+    for w in writes:
+        g.wait_ge(S.qd, w[2])
+        total += send(g, T, topo, core, via if w[3] else dst, mask, slot, rank, w, False)
     g.wait_ge(S.sent, total)
 
 
-def consumer(g, core, T, topo, rank, prods):
+def forwarder(g, core, T, topo, slot, dst, rank, writes, src):
+    arrive = bits(topo.mask(src, dst))
+    mask = topo.mask(core, dst)
+    total = 0
+    for w in writes:
+        if w[3]:
+            g.wait_ge(T.sem["c%d_%d" % (rank, w[1])] if w[0] == "c" else T.sem["p%d" % rank], arrive)
+            total += send(g, T, topo, core, dst, mask, slot, rank, w, True)
+    g.wait_ge(T.sem.sent, total)
+
+
+def consumer(g, core, T, topo, prods, writes, via):
     Copy = ActivationFunctionType.Copy
     S = T.sem
     g.sync.dma_start(T.qb[:], T.q[:]).then_inc(S.ldq, 16)
@@ -101,58 +144,72 @@ def consumer(g, core, T, topo, rank, prods):
     g.vector.wait_ge(S.ldq, 16)
     g.vector.quantize_mx(T.qc[:], T.qs[:], T.qb[:]).then_inc(S.qd, 1)
     g.tensor.wait_ge(S.qd, 1)
-    work = [(None, 0, KO, [(S.ldp, 16), (S.ld0, 16)])]
-    near = [p for p in prods if topo.chip(T.cores[p]) == topo.chip(core)]
-    far = [p for p in prods if p not in near]
-    for group in (near, far):
-        for i, (a, b) in enumerate(PIECES):
-            for p in group:
-                n = 2 * bits(topo.mask(T.cores[p], core))
-                work.append((p, a, b, [(T.sem["a%d_%d" % (p, i)], n)]))
-    nv, ns, stores, u = 0, 0, [0, 0], 0
-    for k, (p, a, b, waits) in enumerate(work):
-        for s, v in waits:
-            g.tensor.wait_ge(s, v)
+    near = [p for p in prods if writes[p] is NEAR]
+    split = [p for p in prods if writes[p] is SPLIT]
+    strt = [p for p in prods if writes[p] is STRAIGHT]
+    work = [(p, c, (0, KO) if c == KO - 1 else None) for p in [None] + near for c in range(KO)]
+    for group, c, run in ((strt, 0, None), (strt, 1, (0, 2)), (split, 0, (0, 1)), (split, 2, (2, 3)), (strt, 2, (2, 3)),
+                          (split, 1, (1, 2))):
+        work += [(p, c, run) for p in group]
+    done, nv, ns, stores = set(), 0, 0, [0, 0]
+
+    def arrived(name, n):
+        if name not in done:
+            done.add(name)
+            g.tensor.wait_ge(T.sem[name], n)
+
+    for u, (p, c, run) in enumerate(work):
         if p is None:
+            arrived("ldp", 16)
+            arrived("ld0", 16)
             kc, ks, base, ybase = T.kcb, T.ksb, 0, 0
         else:
+            for w in writes[p]:
+                if w[1] <= c < w[2]:
+                    n = bits(topo.mask(via[p] if w[3] else T.cores[p], core))
+                    arrived("p%d" % p if w[0] == "p" else "c%d_%d" % (p, w[1]), n)
             kc, ks, base = T.lc, T.ls, W * prods.index(p)
             ybase = W + base
-        for c in range(a, b):
-            if u >= 8:
-                g.tensor.wait_ge(S.vm if u % 2 == 0 else S.sm, (u - 8) // 2 + 1)
-            ps = T["ps%d" % (u % 8)][:, 0:C]
-            cols = slice(base + C * c, base + C * c + C)
-            g.tensor.matmul_mx(ps, T.qc[:], T.qs[:], kc[:, cols], ks[:, cols], True, True).then_inc(S.mm, 1)
-            out = T.yb[:, ybase + C * c:ybase + C * c + C]
-            if u % 2 == 0:
-                g.vector.wait_ge(S.mm, u + 1)
-                g.vector.tensor_copy(out, ps).then_inc(S.vm, 1)
-                nv += 1
-            else:
-                g.scalar.wait_ge(S.mm, u + 1)
-                g.scalar.activation(out, ps, Copy).then_inc(S.sm, 1)
-                ns += 1
-            u += 1
-        j = (u - 1) % 2 if b - a == 1 else k % 2
-        queue = g.scalar if j else g.sync
-        queue.wait_ge(S.vm, nv)
-        queue.wait_ge(S.sm, ns)
-        ycols = slice(ybase + C * a, ybase + C * b)
-        queue.dma_start(T.y[:, ycols], T.yb[:, ycols]).then_inc(S.st1 if j else S.st0, 16)
-        stores[j] += 16
-    g.sync.wait_ge(S.st0, stores[0])
-    g.scalar.wait_ge(S.st1, stores[1])
+        if u >= 8:
+            g.tensor.wait_ge(S.vm if u % 2 == 0 else S.sm, (u - 8) // 2 + 1)
+        ps = T["ps%d" % (u % 8)][:, 0:C]
+        cols = slice(base + C * c, base + C * c + C)
+        g.tensor.matmul_mx(ps, T.qc[:], T.qs[:], kc[:, cols], ks[:, cols], True, True).then_inc(S.mm, 1)
+        out = T.yb[:, ybase + C * c:ybase + C * c + C]
+        if u % 2 == 0:
+            g.vector.wait_ge(S.mm, u + 1)
+            g.vector.tensor_copy(out, ps).then_inc(S.vm, 1)
+            nv += 1
+        else:
+            g.scalar.wait_ge(S.mm, u + 1)
+            g.scalar.activation(out, ps, Copy).then_inc(S.sm, 1)
+            ns += 1
+        if run:
+            j = u % 2
+            queue = g.scalar if j else g.sync
+            queue.wait_ge(S.vm, nv)
+            queue.wait_ge(S.sm, ns)
+            ycols = slice(ybase + C * run[0], ybase + C * run[1])
+            queue.dma_start(T.y[:, ycols], T.yb[:, ycols]).then_inc(S.st1 if j else S.st0, 16)
+            stores[j] += 16
+    for queue, sem, n in ((g.sync, S.st0, stores[0]), (g.scalar, S.st1, stores[1])):
+        if n:
+            queue.wait_ge(sem, n)
 
 
 def rank_program(g, core, T, topo):
-    rank = T.rank_of(core)
-    if rank is None:
-        return
     own = T.tables["OWN"]
-    o = own[rank]
-    prods = [p for p in range(N) if p != o and own[p] == o]
-    if o == rank:
-        consumer(g, core, T, topo, rank, prods)
-    else:
-        producer(g, core, T, topo, prods.index(rank), T.cores[o], rank)
+    rank = T.rank_of(core)
+    for o in range(N):
+        if own[o] != o:
+            continue
+        prods, writes, via = plan(T, topo, o)
+        dst = T.cores[o]
+        if rank == o:
+            consumer(g, core, T, topo, prods, writes, via)
+        elif rank in prods:
+            producer(g, core, T, topo, prods.index(rank), dst, rank, writes[rank], via.get(rank))
+        else:
+            for p, x in via.items():
+                if x == core:
+                    forwarder(g, core, T, topo, prods.index(p), dst, p, writes[p], T.cores[p])

@@ -30,9 +30,10 @@ for _k in range(8):
 SEMAPHORES = ["ld0", "ld1", "ldp", "ldq", "fill", "diag", "sel", "mm", "vm", "sm", "qd", "sent", "st0", "st1"]
 SEMAPHORES += ["c%d_%d" % (_p, _i) for _p in range(N) for _i in range(KO)] + ["p%d" % _p for _p in range(N)]
 
-NEAR = [("c", 0, 3, False), ("p", 0, 3, False)]
-STRAIGHT = [("c", 0, 1, False), ("p", 0, 3, False), ("c", 1, 2, False), ("c", 2, 3, False)]
-SPLIT = [("c", 0, 1, True), ("p", 0, 3, True), ("c", 1, 2, True), ("c", 2, 3, False)]
+NEAR = [("c", 0, 3, None), ("p", 0, 3, None)]
+STRAIGHT = [("c", 0, 1, None), ("p", 0, 3, None), ("c", 1, 2, None), ("c", 2, 3, None)]
+BY_DIE = [("c", 0, 1, "die"), ("p", 0, 3, "die"), ("c", 1, 2, "die"), ("c", 2, 3, "die")]
+BY_BOTH = [("c", 0, 1, "die"), ("c", 1, 2, "mate"), ("p", 0, 3, "mate"), ("c", 2, 3, "mate")]
 
 
 def bits(m):
@@ -44,6 +45,7 @@ def plan(T, topo, o):
     dst = T.cores[o]
     prods = [p for p in range(N) if p != o and own[p] == o]
     writes, via, seen = {}, {}, {}
+    helpers = [x for x in range(SIM) if T.rank_of(x) is None and topo.may_write(x, dst)]
     for p in prods:
         c = T.cores[p]
         if topo.chip(c) == topo.chip(dst):
@@ -52,11 +54,19 @@ def plan(T, topo, o):
         writes[p] = STRAIGHT
         place = (topo.chip(c), topo.die(c))
         seen[place] = seen.get(place, 0) + 1
-        if seen[place] % 2 == 1:
-            free = [x for x in range(SIM) if topo.chip(x) == topo.chip(c) and topo.die(x) != topo.die(c)
-                    and topo.may_write(x, dst) and T.rank_of(x) is None and x not in via.values()]
-            if free:
-                writes[p], via[p] = SPLIT, free[0]
+        if seen[place] % 2 == 0:
+            continue
+        used = list(via.values())
+        free = [x for x in helpers if x not in used]
+        die = [x for x in free if topo.chip(x) == topo.chip(c) and topo.die(x) != topo.die(c)]
+        mate = [x for x in free if topo.mates(topo.chip(x), topo.chip(dst)) and topo.same_plane(topo.chip(x), topo.chip(c))]
+        mate.sort(key=lambda x: len([y for y in used if topo.chip(y) == topo.chip(x) and topo.die(y) == topo.die(x)]))
+        if die:
+            via[p, "die"] = die[0]
+            writes[p] = BY_DIE
+            if mate:
+                via[p, "mate"] = mate[0]
+                writes[p] = BY_BOTH
     return prods, writes, via
 
 
@@ -120,16 +130,16 @@ def producer(g, core, T, topo, slot, dst, rank, writes, via):
     total = 0
     for w in writes:
         g.wait_ge(S.qd, w[2])
-        total += send(g, T, topo, core, via if w[3] else dst, mask, slot, rank, w, False)
+        total += send(g, T, topo, core, via[rank, w[3]] if w[3] else dst, mask, slot, rank, w, False)
     g.wait_ge(S.sent, total)
 
 
-def forwarder(g, core, T, topo, slot, dst, rank, writes, src):
+def forwarder(g, core, T, topo, slot, dst, rank, writes, src, road):
     arrive = bits(topo.mask(src, dst))
     mask = topo.mask(core, dst)
     total = 0
     for w in writes:
-        if w[3]:
+        if w[3] == road:
             g.wait_ge(T.sem["c%d_%d" % (rank, w[1])] if w[0] == "c" else T.sem["p%d" % rank], arrive)
             total += send(g, T, topo, core, dst, mask, slot, rank, w, True)
     g.wait_ge(T.sem.sent, total)
@@ -145,11 +155,11 @@ def consumer(g, core, T, topo, prods, writes, via):
     g.vector.quantize_mx(T.qc[:], T.qs[:], T.qb[:]).then_inc(S.qd, 1)
     g.tensor.wait_ge(S.qd, 1)
     near = [p for p in prods if writes[p] is NEAR]
-    split = [p for p in prods if writes[p] is SPLIT]
+    other = [p for p in prods if writes[p] in (BY_DIE, BY_BOTH)]
     strt = [p for p in prods if writes[p] is STRAIGHT]
     work = [(p, c, (0, KO) if c == KO - 1 else None) for p in [None] + near for c in range(KO)]
-    for group, c, run in ((strt, 0, None), (strt, 1, (0, 2)), (split, 0, (0, 1)), (split, 2, (2, 3)), (strt, 2, (2, 3)),
-                          (split, 1, (1, 2))):
+    for group, c, run in ((strt, 0, None), (strt, 1, (0, 2)), (other, 0, None), (other, 1, (0, 2)), (strt, 2, (2, 3)),
+                          (other, 2, (2, 3))):
         work += [(p, c, run) for p in group]
     done, nv, ns, stores = set(), 0, 0, [0, 0]
 
@@ -166,7 +176,7 @@ def consumer(g, core, T, topo, prods, writes, via):
         else:
             for w in writes[p]:
                 if w[1] <= c < w[2]:
-                    n = bits(topo.mask(via[p] if w[3] else T.cores[p], core))
+                    n = bits(topo.mask(via[p, w[3]] if w[3] else T.cores[p], core))
                     arrived("p%d" % p if w[0] == "p" else "c%d_%d" % (p, w[1]), n)
             kc, ks, base = T.lc, T.ls, W * prods.index(p)
             ybase = W + base
@@ -208,8 +218,8 @@ def rank_program(g, core, T, topo):
         if rank == o:
             consumer(g, core, T, topo, prods, writes, via)
         elif rank in prods:
-            producer(g, core, T, topo, prods.index(rank), dst, rank, writes[rank], via.get(rank))
+            producer(g, core, T, topo, prods.index(rank), dst, rank, writes[rank], via)
         else:
-            for p, x in via.items():
+            for (p, road), x in via.items():
                 if x == core:
-                    forwarder(g, core, T, topo, prods.index(p), dst, p, writes[p], T.cores[p])
+                    forwarder(g, core, T, topo, prods.index(p), dst, p, writes[p], T.cores[p], road)

@@ -40,6 +40,18 @@ def bits(m):
     return bin(m).count("1")
 
 
+def half(mask, k):
+    ones = [i for i in range(mask.bit_length()) if mask >> i & 1]
+    return sum(1 << i for i in ones[k::2])
+
+
+def last_mask(topo, core, dst, k):
+    mask = topo.mask(core, dst)
+    if topo.chip(core) == topo.chip(dst) or k >= 2:
+        return mask
+    return half(mask, k)
+
+
 def plan(T, topo, o):
     own = T.tables["OWN"]
     dst = T.cores[o]
@@ -70,7 +82,7 @@ def plan(T, topo, o):
     return prods, writes, via
 
 
-def send(g, T, topo, core, to, mask, slot, rank, write, landed):
+def send(g, T, topo, to, mask, slot, rank, write, landed):
     kind, a, b, _ = write
     there = slice(W * slot + C * a, W * slot + C * b)
     here = there if landed else slice(C * a, C * b)
@@ -91,10 +103,13 @@ def producer(g, core, T, topo, slot, dst, rank, writes, via):
     g.sync.dma_start(T.kcb[:, 0:C].bitcast(dt.uint8), T.kc[:, 0:4 * C]).then_inc(S.ld0, 16)
     g.scalar.dma_start(T.ksb[:], T.ks[:]).then_inc(S.ldp, 16)
     g.sync.dma_start(T.kcb[:, C:W].bitcast(dt.uint8), T.kc[:, 4 * C:4 * W]).then_inc(S.ld1, 16)
-    g.vector.memset(T.strip[:], 0.0).then_inc(S.fill, 1)
-    g.wait_ge(S.fill, 1)
     d = T.strip[:, 3:515:4]
+    g.vector.memset(d, 0.0).then_inc(S.fill, 1)
+    for k in range(3):
+        g.vector.memset(T.strip[:, k:516:4], 0.0).then_inc(S.fill, 1)
+    g.wait_ge(S.fill, 1)
     g.affine_select(d, d, [[-1, C]], AluOpType.not_equal, 1.0, 0, 1).then_inc(S.diag, 1)
+    g.vector.wait_ge(S.fill, 4)
     g.vector.wait_ge(S.diag, 1)
     order = (0, 2, 1, 3)
     for b in order:
@@ -126,27 +141,24 @@ def producer(g, core, T, topo, slot, dst, rank, writes, via):
         g.vector.wait_ge(S.vm, 2 * (c + 1))
         g.vector.wait_ge(S.sm, 2 * (c + 1))
         g.vector.quantize_mx(T.nc[:, cols], T.ns[:, cols], T.h[:, 4 * C * c:4 * C * (c + 1)]).then_inc(S.qd, 1)
-    mask = topo.mask(core, dst)
     total = 0
-    for w in writes:
+    for k, w in enumerate(writes):
         g.wait_ge(S.qd, w[2])
-        total += send(g, T, topo, core, via[rank, w[3]] if w[3] else dst, mask, slot, rank, w, False)
+        to, mask = (via[rank, w[3]], topo.mask(core, dst)) if w[3] else (dst, last_mask(topo, core, dst, k))
+        total += send(g, T, topo, to, mask, slot, rank, w, False)
     g.wait_ge(S.sent, total)
 
 
 def forwarder(g, core, T, topo, slot, dst, rank, writes, src, road):
     arrive = bits(topo.mask(src, dst))
-    mask = topo.mask(core, dst)
     total = 0
-    for w in writes:
-        if w[3] == road:
-            g.wait_ge(T.sem["c%d_%d" % (rank, w[1])] if w[0] == "c" else T.sem["p%d" % rank], arrive)
-            total += send(g, T, topo, core, dst, mask, slot, rank, w, True)
+    for k, w in enumerate([w for w in writes if w[3] == road]):
+        g.wait_ge(T.sem["c%d_%d" % (rank, w[1])] if w[0] == "c" else T.sem["p%d" % rank], arrive)
+        total += send(g, T, topo, dst, last_mask(topo, core, dst, k), slot, rank, w, True)
     g.wait_ge(T.sem.sent, total)
 
 
 def consumer(g, core, T, topo, prods, writes, via):
-    Copy = ActivationFunctionType.Copy
     S = T.sem
     g.sync.dma_start(T.qb[:], T.q[:]).then_inc(S.ldq, 16)
     g.scalar.dma_start(T.ksb[:], T.ks[:]).then_inc(S.ldp, 16)
@@ -158,10 +170,10 @@ def consumer(g, core, T, topo, prods, writes, via):
     other = [p for p in prods if writes[p] in (BY_DIE, BY_BOTH)]
     strt = [p for p in prods if writes[p] is STRAIGHT]
     work = [(p, c, (0, KO) if c == KO - 1 else None) for p in [None] + near for c in range(KO)]
-    for group, c, run in ((strt, 0, None), (strt, 1, (0, 2)), (other, 0, None), (other, 1, (0, 2)), (strt, 2, (2, 3)),
-                          (other, 2, (2, 3))):
+    for group, c, run in ((strt, 0, None), (strt, 1, (0, 2)), (other, 0, None), (other, 1, (0, 2)), (other, 2, (2, 3)),
+                          (strt, 2, (2, 3))):
         work += [(p, c, run) for p in group]
-    done, nv, ns, stores = set(), 0, 0, [0, 0]
+    done, stores = set(), [0, 0]
 
     def arrived(name, n):
         if name not in done:
@@ -176,29 +188,22 @@ def consumer(g, core, T, topo, prods, writes, via):
         else:
             for w in writes[p]:
                 if w[1] <= c < w[2]:
-                    n = bits(topo.mask(via[p, w[3]] if w[3] else T.cores[p], core))
-                    arrived("p%d" % p if w[0] == "p" else "c%d_%d" % (p, w[1]), n)
+                    sender = via[p, w[3]] if w[3] else T.cores[p]
+                    k = [v for v in writes[p] if v[3] == w[3]].index(w)
+                    arrived("p%d" % p if w[0] == "p" else "c%d_%d" % (p, w[1]), bits(last_mask(topo, sender, core, k)))
             kc, ks, base = T.lc, T.ls, W * prods.index(p)
             ybase = W + base
         if u >= 8:
-            g.tensor.wait_ge(S.vm if u % 2 == 0 else S.sm, (u - 8) // 2 + 1)
+            g.tensor.wait_ge(S.vm, u - 7)
         ps = T["ps%d" % (u % 8)][:, 0:C]
         cols = slice(base + C * c, base + C * c + C)
         g.tensor.matmul_mx(ps, T.qc[:], T.qs[:], kc[:, cols], ks[:, cols], True, True).then_inc(S.mm, 1)
-        out = T.yb[:, ybase + C * c:ybase + C * c + C]
-        if u % 2 == 0:
-            g.vector.wait_ge(S.mm, u + 1)
-            g.vector.tensor_copy(out, ps).then_inc(S.vm, 1)
-            nv += 1
-        else:
-            g.scalar.wait_ge(S.mm, u + 1)
-            g.scalar.activation(out, ps, Copy).then_inc(S.sm, 1)
-            ns += 1
+        g.vector.wait_ge(S.mm, u + 1)
+        g.vector.tensor_copy(T.yb[:, ybase + C * c:ybase + C * c + C], ps).then_inc(S.vm, 1)
         if run:
-            j = u % 2
+            j = 0 if stores[0] <= stores[1] else 1
             queue = g.scalar if j else g.sync
-            queue.wait_ge(S.vm, nv)
-            queue.wait_ge(S.sm, ns)
+            queue.wait_ge(S.vm, u + 1)
             ycols = slice(ybase + C * run[0], ybase + C * run[1])
             queue.dma_start(T.y[:, ycols], T.yb[:, ycols]).then_inc(S.st1 if j else S.st0, 16)
             stores[j] += 16

from concourse.mybir import dt, AluOpType, ActivationFunctionType

N = 8
KO = 3
C = 128
W = KO * C
SIM = 128
FAC = 0.800000011920929
X4 = "float8_e4m3fn_x4"

SCRATCH = {
    "kcb": ("sbuf", [128, W], X4),
    "ksb": ("sbuf", [128, W], "uint8"),
    "strip": ("sbuf", [128, 516], "bfloat16"),
    "sc": ("sbuf", [128, 4 * C], X4),
    "ss": ("sbuf", [128, 4 * C], "uint8"),
    "h": ("sbuf", [128, 4 * W], "bfloat16"),
    "nc": ("sbuf", [128, W], X4),
    "ns": ("sbuf", [128, W], "uint8"),
    "lc": ("sbuf", [128, (N - 1) * W], X4),
    "ls": ("sbuf", [128, (N - 1) * W], "uint8"),
    "qb": ("sbuf", [128, 4 * C], "bfloat16"),
    "qc": ("sbuf", [128, C], X4),
    "qs": ("sbuf", [128, C], "uint8"),
    "yb": ("sbuf", [128, N * W], "float32"),
}
for _k in range(8):
    SCRATCH["ps%d" % _k] = ("psum", [128, 512], "float32")

SEMAPHORES = ["ld0", "ld1", "ldp", "ldq", "fill", "diag", "sel", "mm", "vm", "sm", "qd", "sent", "st0", "st1"]
SEMAPHORES += ["c%d_%d" % (_p, _i) for _p in range(N) for _i in range(KO)] + ["p%d" % _p for _p in range(N)]

NEAR = [("c", 0, 3, None), ("p", 0, 3, None)]
STRAIGHT = [("c", 0, 1, None), ("p", 0, 3, None), ("c", 1, 2, None), ("c", 2, 3, None)]
BY_DIE = [("c", 0, 1, "die"), ("p", 0, 3, "die"), ("c", 1, 2, "die"), ("c", 2, 3, "die")]
BY_BOTH = [("c", 0, 1, "die"), ("c", 1, 2, "mate"), ("p", 0, 3, "mate"), ("c", 2, 3, "mate")]


def bits(m):
    return bin(m).count("1")


def half(mask, k):
    ones = [i for i in range(mask.bit_length()) if mask >> i & 1]
    return sum(1 << i for i in ones[k::2])


def last_mask(topo, core, dst, k):
    mask = topo.mask(core, dst)
    if topo.chip(core) == topo.chip(dst) or k >= 2:
        return mask
    return half(mask, k)


def plan(T, topo, o):
    own = T.tables["OWN"]
    dst = T.cores[o]
    prods = [p for p in range(N) if p != o and own[p] == o]
    writes, via, seen = {}, {}, {}
    helpers = [x for x in range(SIM) if T.rank_of(x) is None and topo.may_write(x, dst)]
    for p in prods:
        c = T.cores[p]
        if topo.chip(c) == topo.chip(dst):
            writes[p] = NEAR
            continue
        writes[p] = STRAIGHT
        place = (topo.chip(c), topo.die(c))
        seen[place] = seen.get(place, 0) + 1
        if seen[place] % 2 == 0:
            continue
        used = list(via.values())
        free = [x for x in helpers if x not in used]
        die = [x for x in free if topo.chip(x) == topo.chip(c) and topo.die(x) != topo.die(c)]
        mate = [x for x in free if topo.mates(topo.chip(x), topo.chip(dst)) and topo.same_plane(topo.chip(x), topo.chip(c))]
        mate.sort(key=lambda x: len([y for y in used if topo.chip(y) == topo.chip(x) and topo.die(y) == topo.die(x)]))
        if die:
            via[p, "die"] = die[0]
            writes[p] = BY_DIE
            if mate:
                via[p, "mate"] = mate[0]
                writes[p] = BY_BOTH
    return prods, writes, via


def send(g, T, topo, to, mask, slot, rank, write, landed):
    kind, a, b, _ = write
    there = slice(W * slot + C * a, W * slot + C * b)
    here = there if landed else slice(C * a, C * b)
    rid, pid, _ = topo.addr(to)
    if kind == "c":
        src = T.lc if landed else T.nc
        out, in_, sem = T.lc[:, there].bitcast(dt.uint8), src[:, here].bitcast(dt.uint8), T.sem["c%d_%d" % (rank, a)]
    else:
        src = T.ls if landed else T.ns
        out, in_, sem = T.ls[:, there], src[:, here], T.sem["p%d" % rank]
    g.remote_dma(out_ap=out, in_ap=in_, remote_sem=sem, local_sem=T.sem.sent, pid=pid, routing_id=rid, dma_engine_mask=mask)
    return bits(mask)


def producer(g, core, T, topo, slot, dst, rank, writes, via):
    Copy = ActivationFunctionType.Copy
    S = T.sem
    g.sync.dma_start(T.kcb[:, 0:C].bitcast(dt.uint8), T.kc[:, 0:4 * C]).then_inc(S.ld0, 16)
    g.scalar.dma_start(T.ksb[:], T.ks[:]).then_inc(S.ldp, 16)
    g.sync.dma_start(T.kcb[:, C:W].bitcast(dt.uint8), T.kc[:, 4 * C:4 * W]).then_inc(S.ld1, 16)
    d = T.strip[:, 3:515:4]
    g.vector.memset(d, 0.0).then_inc(S.fill, 1)
    for k in range(3):
        g.vector.memset(T.strip[:, k:516:4], 0.0).then_inc(S.fill, 1)
    g.wait_ge(S.fill, 1)
    g.affine_select(d, d, [[-1, C]], AluOpType.not_equal, 1.0, 0, 1).then_inc(S.diag, 1)
    g.vector.wait_ge(S.fill, 4)
    g.vector.wait_ge(S.diag, 1)
    order = (0, 2, 1, 3)
    for b in order:
        g.vector.quantize_mx(T.sc[:, C * b:C * b + C], T.ss[:, C * b:C * b + C], T.strip[:, 3 - b:515 - b]).then_inc(S.sel, 1)
    for c in range(KO):
        if c == 0:
            g.tensor.wait_ge(S.ld0, 16)
            g.tensor.wait_ge(S.ldp, 16)
        if c == 1:
            g.tensor.wait_ge(S.ld1, 16)
        if c >= 2:
            g.tensor.wait_ge(S.vm, 2 * (c - 1))
            g.tensor.wait_ge(S.sm, 2 * (c - 1))
        cols = slice(C * c, C * c + C)
        for k, b in enumerate(order):
            if c == 0:
                g.tensor.wait_ge(S.sel, k + 1)
            g.tensor.matmul_mx(T["ps%d" % (4 * (c % 2) + b)][:, 0:C], T.sc[:, C * b:C * b + C], T.ss[:, C * b:C * b + C],
                               T.kcb[:, cols], T.ksb[:, cols], True, True).then_inc(S.mm, 1)
        for k, b in enumerate(order):
            src = T["ps%d" % (4 * (c % 2) + b)][:, 0:C]
            out = T.h[:, 4 * C * c + b:4 * C * (c + 1):4]
            if b < 2:
                g.scalar.wait_ge(S.mm, 4 * c + k + 1)
                g.scalar.activation(out, src, Copy, scale=FAC).then_inc(S.sm, 1)
            else:
                g.vector.wait_ge(S.mm, 4 * c + k + 1)
                g.vector.tensor_scalar(out, src, FAC, None, AluOpType.mult).then_inc(S.vm, 1)
        g.vector.wait_ge(S.vm, 2 * (c + 1))
        g.vector.wait_ge(S.sm, 2 * (c + 1))
        g.vector.quantize_mx(T.nc[:, cols], T.ns[:, cols], T.h[:, 4 * C * c:4 * C * (c + 1)]).then_inc(S.qd, 1)
    total = 0
    for k, w in enumerate(writes):
        g.wait_ge(S.qd, w[2])
        to, mask = (via[rank, w[3]], topo.mask(core, dst)) if w[3] else (dst, last_mask(topo, core, dst, k))
        total += send(g, T, topo, to, mask, slot, rank, w, False)
    g.wait_ge(S.sent, total)


def forwarder(g, core, T, topo, slot, dst, rank, writes, src, road):
    arrive = bits(topo.mask(src, dst))
    total = 0
    for k, w in enumerate([w for w in writes if w[3] == road]):
        g.wait_ge(T.sem["c%d_%d" % (rank, w[1])] if w[0] == "c" else T.sem["p%d" % rank], arrive)
        total += send(g, T, topo, dst, last_mask(topo, core, dst, k), slot, rank, w, True)
    g.wait_ge(T.sem.sent, total)


def consumer(g, core, T, topo, prods, writes, via):
    S = T.sem
    g.sync.dma_start(T.qb[:], T.q[:]).then_inc(S.ldq, 16)
    g.scalar.dma_start(T.ksb[:], T.ks[:]).then_inc(S.ldp, 16)
    g.sync.dma_start(T.kcb[:].bitcast(dt.uint8), T.kc[:]).then_inc(S.ld0, 16)
    g.vector.wait_ge(S.ldq, 16)
    g.vector.quantize_mx(T.qc[:], T.qs[:], T.qb[:]).then_inc(S.qd, 1)
    g.tensor.wait_ge(S.qd, 1)
    near = [p for p in prods if writes[p] is NEAR]
    other = [p for p in prods if writes[p] in (BY_DIE, BY_BOTH)]
    strt = [p for p in prods if writes[p] is STRAIGHT]
    work = [(p, c, (0, KO) if c == KO - 1 else None) for p in [None] + near for c in range(KO)]
    for group, c, run in ((strt, 0, None), (strt, 1, (0, 2)), (other, 0, None), (other, 1, (0, 2)), (other, 2, (2, 3)),
                          (strt, 2, (2, 3))):
        work += [(p, c, run) for p in group]
    done, stores = set(), [0, 0]

    def arrived(name, n):
        if name not in done:
            done.add(name)
            g.tensor.wait_ge(T.sem[name], n)

    for u, (p, c, run) in enumerate(work):
        if p is None:
            arrived("ldp", 16)
            arrived("ld0", 16)
            kc, ks, base, ybase = T.kcb, T.ksb, 0, 0
        else:
            for w in writes[p]:
                if w[1] <= c < w[2]:
                    sender = via[p, w[3]] if w[3] else T.cores[p]
                    k = [v for v in writes[p] if v[3] == w[3]].index(w)
                    arrived("p%d" % p if w[0] == "p" else "c%d_%d" % (p, w[1]), bits(last_mask(topo, sender, core, k)))
            kc, ks, base = T.lc, T.ls, W * prods.index(p)
            ybase = W + base
        if u >= 8:
            g.tensor.wait_ge(S.vm, u - 7)
        ps = T["ps%d" % (u % 8)][:, 0:C]
        cols = slice(base + C * c, base + C * c + C)
        g.tensor.matmul_mx(ps, T.qc[:], T.qs[:], kc[:, cols], ks[:, cols], True, True).then_inc(S.mm, 1)
        g.vector.wait_ge(S.mm, u + 1)
        g.vector.tensor_copy(T.yb[:, ybase + C * c:ybase + C * c + C], ps).then_inc(S.vm, 1)
        if run:
            j = 0 if stores[0] <= stores[1] else 1
            queue = g.scalar if j else g.sync
            queue.wait_ge(S.vm, u + 1)
            ycols = slice(ybase + C * run[0], ybase + C * run[1])
            queue.dma_start(T.y[:, ycols], T.yb[:, ycols]).then_inc(S.st1 if j else S.st0, 16)
            stores[j] += 16
    for queue, sem, n in ((g.sync, S.st0, stores[0]), (g.scalar, S.st1, stores[1])):
        if n:
            queue.wait_ge(sem, n)


def rank_program(g, core, T, topo):
    own = T.tables["OWN"]
    rank = T.rank_of(core)
    for o in range(N):
        if own[o] != o:
            continue
        prods, writes, via = plan(T, topo, o)
        dst = T.cores[o]
        if rank == o:
            consumer(g, core, T, topo, prods, writes, via)
        elif rank in prods:
            producer(g, core, T, topo, prods.index(rank), dst, rank, writes[rank], via)
        else:
            for (p, road), x in via.items():
                if x == core:
                    forwarder(g, core, T, topo, prods.index(p), dst, p, writes[p], T.cores[p], road)
